import numpy as np, ml_dtypes
CORES = [3,7,11,15,131,135,139,143]
N = 8
BF = ml_dtypes.bfloat16
def gentries(a):
    return np.ascontiguousarray(a.reshape(8, 16, -1).transpose(0, 2, 1)).reshape(8, -1)
def gtable(e):
    e = np.asarray(e); return np.ascontiguousarray(e.reshape(8, -1, 16).transpose(0, 2, 1)).reshape(128, -1).astype(np.int32)
def f(rng, *shape):
    return (rng.standard_normal(shape, dtype=np.float32) * np.exp2(rng.integers(-2, 3, shape[:-1] + (1,)))).astype(BF)
def wide(rng, *shape):
    v = f(rng, *shape).astype(np.float32); k = shape[:-2] + (1, shape[-1])
    return (v * np.exp2(rng.integers(-6, 7, k)) * (rng.random(k) > 0.0625)).astype(BF)
LV, M, S = 3, 704, 32
R, A = LV * M, (LV - 1) * (N - 1) * S
W, K = R + A, 4 * M * (LV - 1)
LEV4 = np.repeat(np.concatenate([np.arange(R) // M, np.arange(A) // ((N - 1) * S)]), 4)
OWN4 = np.repeat(np.arange(W) < R, 4).astype(np.float64)
def draw_ent(rng, pri, tidy):
    e = np.zeros((8, LV - 1, 4, M), np.int64)
    for g in range(8):
        free = np.ones(4 * W, bool)
        for l in range(1, LV):
            c = np.flatnonzero(free & (LEV4 < l)); c = c[np.argsort(pri[c] + rng.random(len(c)))[:4 * M]]; free[c] = False
            e[g, l - 1] = np.sort(c).reshape(M, 4)[rng.permutation(M)].T if tidy else rng.permutation(c).reshape(4, M)
    return gtable(e.reshape(8, -1))
def draw_sl(rng, same):
    s = np.zeros((8, LV - 1, N - 1, S), np.int64)
    for g in range(8):
        for l in range(LV - 1):
            if same:
                u = np.concatenate([[0, M - 1], 1 + rng.permutation(M - 2)[:S - 2]]); v = [rng.permutation(u) for d in range(N - 1)]
            else:
                v = [rng.permutation(M)[:S] for d in range(N - 1)]
            s[g, l] = l * M + np.stack(v)
    return gtable(s.reshape(8, -1))
def draw(rng, pri, tidy, same):
    return {"b": f(rng, N, 128, R), "val": ((rng.random((N, 8, K)) - 0.5) * 0.5).astype(BF),
            "ent": np.stack([draw_ent(rng, pri[r], tidy[r]) for r in range(N)]), "sl": np.stack([draw_sl(rng, same) for r in range(N)])}
def setup_inputs(rng):
    return draw(rng, [0 * OWN4] * N, [False] * N, False)
def setup_inputs_same(rng):
    return draw(rng, [OWN4] * N, [False] * N, True)
def setup_inputs_old(rng):
    return draw(rng, [LEV4.astype(np.float64)] * N, [False] * N, False)
def setup_inputs_mixed(rng):
    o = int(rng.integers(0, 2))
    return draw(rng, [1 - OWN4 if (r + o) % 2 else OWN4 for r in range(N)], [(r + o) % 2 == 1 for r in range(N)], False)
def setup_inputs_strong(rng):
    d = setup_inputs(rng); d["val"] = np.where(rng.random((N, 8, K)) < 0.9, -0.25, 0.25).astype(BF); return d
def setup_inputs_spread(rng):
    d = setup_inputs(rng); d["b"] = wide(rng, N, 128, R)
    d["val"] = (d["val"].astype(np.float32) * np.exp2(-rng.integers(0, 7, (N, 8, K))) * (rng.random((N, 8, K)) > 0.0625)).astype(BF); return d
def check_inputs(d):
    bad = []
    if not np.isfinite(d["b"].astype(np.float32)).all(): bad.append("b finite")
    if not (np.abs(d["val"].astype(np.float32)) <= 0.25).all(): bad.append("size of val")
    lv = np.arange(LV - 1)
    for r in range(N):
        e = gentries(d["ent"][r]).astype(np.int64); s = gentries(d["sl"][r]).astype(np.int64).reshape(8, LV - 1, N - 1, S)
        if (e < 0).any() or (e >= 4 * W).any(): bad.append("ent range")
        elif (LEV4[e].reshape(8, LV - 1, 4 * M) > lv[:, None]).any(): bad.append("ent level")
        if (np.diff(np.sort(e, axis=1), axis=1) == 0).any(): bad.append("ent differ")
        if (s // M != lv[:, None, None]).any(): bad.append("sl level")
        if (np.diff(np.sort(s, axis=3), axis=3) == 0).any(): bad.append("sl differ")
    return sorted(set(bad))
def reference(b, val, ent, sl):
    en = np.stack([gentries(ent[r]) for r in range(N)]).astype(np.int64).reshape(N, 8, LV - 1, 4, M); place = en // 4
    se = np.stack([gentries(sl[r]) for r in range(N)]).astype(np.int64).reshape(N, 8, LV - 1, N - 1, S)
    v = val.astype(np.float64).reshape(N, 8, LV - 1, 4, M)
    w = np.zeros((N, 8, 16, W), np.float64); w[..., :R] = b.astype(np.float64).reshape(N, 8, 16, R)
    for l in range(LV):
        for r in range(N):
            for g in range(8):
                if l > 0: w[r, g, :, l * M:(l + 1) * M] -= np.sum(v[r, g, l - 1] * w[r, g][:, place[r, g, l - 1]], axis=1)
                if l < LV - 1:
                    for d in range(N - 1):
                        m = R + (l * (N - 1) + d) * S
                        w[(r + 1 + d) % N, g, :, m:m + S] = w[r, g][:, se[r, g, l, d]]
    z = np.zeros((N, 8, 16, R), np.float64); bk = np.zeros((N, 8, 16, 4 * W), np.float64)
    for l in range(LV - 1, -1, -1):
        for r in range(N):
            for g in range(8):
                x = w[r, g, :, l * M:(l + 1) * M] - np.sum(bk[r, g, :, 4 * l * M:4 * (l + 1) * M].reshape(16, M, 4), axis=2)
                if l < LV - 1:
                    for d in range(N - 1):
                        m = R + (l * (N - 1) + d) * S
                        x[:, se[r, g, l, d] - l * M] -= np.sum(bk[(r + 1 + d) % N, g, :, 4 * m:4 * (m + S)].reshape(16, S, 4), axis=2)
                z[r, g, :, l * M:(l + 1) * M] = x
                if l > 0: bk[r, g][:, en[r, g, l - 1]] = v[r, g, l - 1] * x[:, None, :]
    return {"z": z.reshape(N, 128, R).astype(np.float32)}

@@ -1,0 +1,476 @@
+from concourse.bass import DstId, RemoteDMATransfer
+from concourse.mybir import AluOpType, ActivationFunctionType
+
+N, M, S = 8, 704, 32
+R, GH = 3 * M, 7 * S
+K4 = 4 * M
+PAD = 32
+V2, V1 = PAD, PAD + K4
+ROW = 640
+NPE = 2
+SHOWN_FIRST = True
+GHOST_DIRECT = True
+TWO_CALLS = True
+VCV = 4
+CONV = "s"
+SHARE = M
+
+SCRATCH = {
+    "wb": ("sbuf", [128, R + GH], "bfloat16"),
+    "w": ("sbuf", [128, R + 2 * GH], "float32"),
+    "valb": ("sbuf", [128, PAD + 2 * K4], "bfloat16"),
+    "pw": ("sbuf", [128, PAD + 2 * K4], "float32"),
+    "num": ("sbuf", [128, 2 * K4], "float32"),
+    "inva": ("sbuf", [128, 16 * ROW], "float32"),
+    "invb": ("sbuf", [128, 16 * ROW], "float32"),
+    "ext": ("sbuf", [128, ROW], "float32"),
+    "exb": ("sbuf", [128, ROW], "float32"),
+    "lk1": ("sbuf", [128, M + 6 * S], "float32"),
+    "lk0": ("sbuf", [128, M + 6 * S], "float32"),
+    "lu": ("sbuf", [128, 112], "uint16"),
+    "enti": ("sbuf", [128, 352], "int32"),
+    "pl": ("sbuf", [128, 352], "int32"),
+    "plu": ("sbuf", [128, 352], "uint16"),
+    "qa": ("sbuf", [128, 352], "int32"),
+    "qb": ("sbuf", [128, 352], "float32"),
+    "qu": ("sbuf", [128, 352], "uint16"),
+    "sli": ("sbuf", [128, 28], "int32"),
+    "si": ("sbuf", [128, 32], "int32"),
+    "so": ("sbuf", [128, 84], "uint16"),
+    "ci": ("sbuf", [128, 152], "int32"),
+    "cj": ("sbuf", [128, 24], "int32"),
+    "eq": ("sbuf", [128, 16], "float32"),
+    "sel": ("sbuf", [128, 144], "float32"),
+    "idb": ("sbuf", [128, 128], "bfloat16"),
+    "idn": ("sbuf", [128, 128], "float32"),
+    "idp": ("sbuf", [128, 128], "float32"),
+    "msk": ("sbuf", [128, GH], "float32"),
+    "gm": ("sbuf", [128, 4 * GH], "float32"),
+    "pcu": ("sbuf", [128, 56], "uint16"),
+    "vc": ("sbuf", [128, 4 * GH], "bfloat16"),
+    "vg": ("sbuf", [128, 4 * GH], "bfloat16"),
+    "bsh": ("sbuf", [128, GH], "bfloat16"),
+    "pr": ("sbuf", [128, K4], "float32"),
+    "ps": ("sbuf", [128, 4 * GH], "float32"),
+    "x1": ("sbuf", [128, GH], "bfloat16"),
+    "x2": ("sbuf", [128, GH], "float32"),
+    "x3": ("sbuf", [128, GH], "float32"),
+    "x4": ("sbuf", [128, GH], "float32"),
+    "r3": ("sbuf", [128, PAD + GH], "float32"),
+    "r4": ("sbuf", [128, PAD + GH], "float32"),
+    "og": ("sbuf", [128, 112], "uint16"),
+    "oo": ("sbuf", [128, 352], "uint16"),
+    "gn": ("sbuf", [128, 168], "float32"),
+    "gk": ("sbuf", [128, 56], "int32"),
+    "xu": ("sbuf", [128, 56], "uint16"),
+    "zw": ("sbuf", [128, 2 * M], "float32"),
+    "z0": ("sbuf", [128, M], "float32"),
+    "acc1": ("psum", [128, 1024], "float32"),
+    "acc2": ("psum", [128, 1024], "float32"),
+    "accs": ("psum", [128, 512], "float32"),
+    "accp": ("psum", [128, 512], "float32"),
+    "accq": ("psum", [128, 512], "float32"),
+    "accr": ("psum", [128, 512], "float32"),
+}
+DMA_SEMS = ["d_sl", "d_b0", "d_ent", "d_fa", "d_fb", "d_v1", "d_v2", "d_b12", "d_e1", "d_e0", "d_z2", "d_z1", "d_z0", "d_z0b"]
+OWN_SEMS = ["s_v", "s_s", "s_t", "s_g"]
+SEMAPHORES = OWN_SEMS + ["arr%d" % k for k in range(1, 5)] + ["snt%d%s" % (k, c) for k in range(1, 5) for c in "ab"] + DMA_SEMS
+PSUM = ("acc1", "acc2", "accs", "accp", "accq", "accr")
+ALU, ACT = AluOpType, ActivationFunctionType
+
+
+def calls_of(T, topo, r, back):
+    src = T.cores[r]
+    on, off = [], []
+    for d in range(N - 1):
+        q = (r - 1 - d) % N if back else (r + 1 + d) % N
+        (on if T.cores[q] in topo.cores_of(src) else off).append((d, q))
+    off.sort(key=lambda x: (topo.mates(src, T.cores[x[1]]), topo.same_plane(src, T.cores[x[1]])))
+    eo = topo.engines(src, T.cores[off[0][1]])
+    ei = [e for e in topo.engines(src, T.cores[on[0][1]]) if e not in eo]
+
+    def mask(es):
+        return sum(1 << e for e in es)
+    if not TWO_CALLS:
+        return [[(d, q, mask([eo[i]])) for i, (d, q) in enumerate(off)] + [(on[0][0], on[0][1], mask(ei[:1]))]]
+    a, b = len(eo) // 4, len(eo) // 2
+    first = [(d, q, mask(eo[a * i:a * i + a])) for i, (d, q) in enumerate(off[:4])] + [(on[0][0], on[0][1], mask(ei[:2]))]
+    second = [(d, q, mask(eo[b * i:b * i + b])) for i, (d, q) in enumerate(off[4:])]
+    return [first, second]
+
+
+def bits(m):
+    return bin(m).count("1")
+
+
+def emit(g, T, ops):
+    queues = {"v": g.vector, "s": g.scalar, "t": g.tensor, "g": g, "y": g.sync}
+    total, count = {}, {}
+    for o in ops:
+        if o["sem"] not in OWN_SEMS:
+            total[o["sem"]] = total.get(o["sem"], 0) + o["inc"]
+    known = {q: {} for q in queues}
+    for i, o in enumerate(ops):
+        own = o["sem"] not in total
+        if own:
+            count[o["sem"]] = count.get(o["sem"], 0) + 1
+        o["tok"] = count[o["sem"]] if own else total[o["sem"]]
+        if o["q"] is None:
+            o["clock"] = {}
+            continue
+        kn = known[o["q"]]
+        deps = list(o["after"])
+        for p in ops[:i]:
+            if p["sem"] == o["sem"] and not own:
+                continue
+            hit = False
+            for (b1, l1, h1, w1) in o["acc"]:
+                for (b2, l2, h2, w2) in p["acc"]:
+                    if b1 != b2:
+                        continue
+                    if b1 in PSUM and o["q"] != p["q"]:
+                        hit = True
+                    elif l1 < h2 and l2 < h1 and (w1 or w2) and not (b1 in PSUM and o["q"] == "t"):
+                        hit = True
+            if hit:
+                deps.append(p)
+        for p in reversed(deps):
+            if kn.get(p["sem"], 0) < p["tok"]:
+                queues[o["q"]].wait_ge(T.sem[p["sem"]], p["tok"])
+                kn[p["sem"]] = p["tok"]
+                for s, c in p["clock"].items():
+                    kn[s] = max(kn.get(s, 0), c)
+        o["clock"] = dict(kn)
+        ins = o["fn"](queues[o["q"]])
+        if o["then"]:
+            ins.then_inc(T.sem[o["sem"]], o["inc"])
+    for s, c in list(count.items()) + list(total.items()):
+        if max(known[q].get(s, 0) for q in known) < c:
+            g.wait_ge(T.sem[s], c)
+
+
+def rank_program(g, core, T, topo):
+    rank = T.rank_of(core)
+    if rank is None:
+        return
+    ops = []
+
+    def A(name, lo, hi, step=1):
+        return (T[name][:, lo:hi] if step == 1 else T[name][:, lo:hi:step], [(name, lo, hi)])
+
+    def I(win, off):
+        return (win[0].indirect(off[0]), win[1], off[1])
+
+    def rec(q, sem, inc, fn, outs, ins, then=True, after=()):
+        acc = []
+        for x in outs:
+            acc += [r + (True,) for r in x[1]] + ([r + (False,) for r in x[2]] if len(x) > 2 else [])
+        for x in ins:
+            acc += [r + (False,) for r in x[1]] + ([r + (False,) for r in x[2]] if len(x) > 2 else [])
+        o = {"q": q, "sem": sem, "inc": inc, "fn": fn, "acc": acc, "then": then, "after": list(after)}
+        ops.append(o)
+        return o
+
+    def copy(out, a):
+        return rec("v", "s_v", 1, lambda e: e.tensor_copy(out[0], a[0]), [out], [a])
+
+    def tt(out, a, b, op):
+        return rec("v", "s_v", 1, lambda e: e.tensor_tensor(out[0], a[0], b[0], op), [out], [a, b])
+
+    def ts(out, a, s1, op0, s2=None, op1=None):
+        if s2 is None:
+            return rec("v", "s_v", 1, lambda e: e.tensor_scalar(out[0], a[0], s1, None, op0), [out], [a])
+        return rec("v", "s_v", 1, lambda e: e.tensor_scalar(out[0], a[0], s1, s2, op0, op1), [out], [a])
+
+    def fill(out, c):
+        return rec("v", "s_v", 1, lambda e: e.memset(out[0], c), [out], [])
+
+    def act(out, a, func, scale=None):
+        if scale is None:
+            return rec("s", "s_s", 1, lambda e: e.activation(out[0], a[0], func), [out], [a])
+        return rec("s", "s_s", 1, lambda e: e.activation(out[0], a[0], func, scale=scale), [out], [a])
+
+    def mm(out, lhs, rhs, start, stop):
+        return rec("t", "s_t", 1, lambda e: e.matmul(out[0], lhs[0], rhs[0], start, stop), [out], [lhs, rhs])
+
+    def iota(out, pattern, base, cm, flt=False):
+        if flt:
+            return rec("g", "s_g", 1, lambda e: e.iota(out[0], pattern, base, cm, allow_small_or_imprecise_dtypes=True), [out], [])
+        return rec("g", "s_g", 1, lambda e: e.iota(out[0], pattern, base, cm), [out], [])
+
+    def dma(q, sem, out, a, after=()):
+        return rec(q, sem, 16, lambda e: e.dma_start(out[0], a[0]), [out], [a], after=after)
+
+    def hbm(ap):
+        return (ap, [])
+
+    def exchange(k, src, dst, col, back):
+        sent = []
+        for call, tag in zip(calls_of(T, topo, rank, back), "ab"):
+            trs = []
+            for (d, q, m) in call:
+                rid, pid = topo.addr(T.cores[q], core)
+                trs.append(RemoteDMATransfer(dst_ids=[DstId(rid=rid, pnc=pid)], dma_engine_mask=m, remote_sem=T.sem["arr%d" % k],
+                                             src=T[src][:, S * d:S * d + S], dst=T[dst][:, col + S * d:col + S * d + S]))
+            name = "snt%d%s" % (k, tag)
+            sent.append(rec("g", name, sum(bits(m) for (d, q, m) in call),
+                            lambda e, trs=trs, name=name: e.remote_dma_fused(trs, local_sem=T.sem[name]), [], [A(src, 0, GH)], then=False))
+        n = sum(bits(m) for r in range(N) for call in calls_of(T, topo, r, back) for (d, q, m) in call if q == rank)
+        rec(None, "arr%d" % k, n, None, [A(dst, col, col + GH)], [])
+        return sent[0]
+
+    def spread(q, sem, c, lvl, after=()):
+        col = V1 if lvl == 1 else V2
+        return dma(q, sem, (T.valb[c:128:16, col:col + K4], [("valb", col, col + K4)]), hbm(T.val[:, (lvl - 1) * K4:lvl * K4]), after=after)
+
+    def rows(name):
+        return (T[name][0:128:16, :], [(name, 0, 16 * ROW)])
+
+    def banks(n):
+        return [(lo, min(lo + 512, n)) for lo in range(0, n, 512)]
+
+    def sub(x, lo, hi):
+        return A(x[0], x[1] + lo, x[1] + hi)
+
+    def level(n, win, off, fac, prod, acc, base, out, sign):
+        ident = A("idn" if sign < 0 else "idp", 0, 128)
+        op = ALU.subtract if sign < 0 else ALU.add
+        if base is not None:
+            for lo, hi in banks(n):
+                mm(A(acc, lo, hi), A("idb", 0, 128), sub(base, lo, hi), True, False)
+        for e in range(4):
+            tt(sub(prod[e], 0, n), I(win, off(e)), fac(e), ALU.mult)
+            if e < NPE:
+                for lo, hi in banks(n):
+                    mm(A(acc, lo, hi), ident, sub(prod[e], lo, hi), base is None and e == 0, e == NPE - 1)
+        for e in range(NPE, 3):
+            tt(A(acc, 0, n), A(acc, 0, n), sub(prod[e], 0, n), op)
+        if out is None:
+            tt(A(acc, 0, n), sub(prod[3], 0, n), A(acc, 0, n), ALU.subtract)
+        else:
+            tt(out, A(acc, 0, n), sub(prod[3], 0, n), op)
+
+    def positions(lo, hi, between):
+        ts(A("qa", lo, hi), A("enti", lo, hi), 63, ALU.bitwise_and)
+        between[0]()
+        ts(A("qb", lo, hi), A("qa", lo, hi), float(64 * 160 - 1), ALU.mult)
+        between[1]()
+        tt(A("qb", lo, hi), A("qb", lo, hi), A("enti", lo, hi), ALU.add)
+        between[2]()
+        ts(A("qu", lo, hi), A("qb", lo, hi), 1.0 / 64, ALU.mult)
+
+    def numbers(k):
+        iota(A("num", M * k, M * k + M), [[1, M]], PAD + M * k, 0, True)
+
+    def invert(k, between):
+        col = (176 + 44 * k) if k < 4 else 44 * (k - 4)
+        for lo, hi in ((0, 22), (22, 44)) if between else ((0, 44),):
+            act(I(A("inva" if k < 4 else "invb", 0, 16 * ROW), A("qu", col + lo, col + hi)), A("num", M * k + 16 * lo, M * k + 16 * hi), ACT.Silu)
+            if between:
+                between.pop(0)()
+
+    def pack(acc, block, width, srcs):
+        for s in range(4):
+            for k, src in enumerate(srcs):
+                mm(A(acc, width * s, width * s + width), A("idp", 0, 128), A(src, 160 * s + block, 160 * s + block + width),
+                   k == 0, k == len(srcs) - 1)
+
+    def deal(acc, src):
+        for c in range(16):
+            mm(A(acc, 0, 56), A("sel", 15 - c, 143 - c), A(src, c, 4 * GH, 16), c == 0, c == 15)
+
+    def links(lk, col):
+        steps = []
+        for d in range(N - 1):
+            o = A("so", col + 2 * d, col + 2 * d + 2)
+            if d:
+                steps.append(lambda d=d, o=o: act(A(lk, M + S * (d - 1), M + S * d), I(A(lk, 0, M), o), ACT.Copy))
+            steps.append(lambda d=d, o=o: act(I(A(lk, 0, M), o), A("num", S * d, S * d + S), ACT.Silu))
+        return steps
+
+    def products(col, acc):
+        for e in range(4):
+            tt(A("pw", col + M * e, col + M * e + M), A("valb", col + M * e, col + M * e + M), A(acc, 0, M), ALU.mult)
+
+    def slot(out, win, off, base):
+        if base is None:
+            copy(out, I(win, off))
+        else:
+            tt(out, I(win, off), base, ALU.add)
+
+    def slots(out, win, off, col, width, base, n=4, between=()):
+        for s in range(n):
+            slot(out, win, A(off, col + s * width, col + (s + 1) * width), base if s == 0 else out)
+            if s < len(between):
+                between[s]()
+
+    def chain(rc, col, between=()):
+        for d in range(1, N - 1):
+            x = A(rc, PAD + S * d, PAD + S * d + S)
+            tt(x, I(A(rc, 0, PAD + S * d), A("lu", col + 42 + 2 * d, col + 44 + 2 * d)), x, ALU.add)
+            if d - 1 < len(between):
+                between[d - 1]()
+
+    def last(rc, col, z, lo, hi):
+        tt(sub(z, lo, hi), I(A(rc, 0, PAD + GH), A("lu", col + lo // 16, col + hi // 16)), sub(z, lo, hi), ALU.add)
+
+    dma("y", "d_sl", A("sli", 0, 28), hbm(T.sl[:]))
+    dma("s", "d_b0", A("wb", 0, M), hbm(T.b[:, 0:M]))
+    dma("y", "d_ent", A("enti", 0, 352), hbm(T.ent[:]))
+    zeros = fill(A("lk0", 0, M), 0.0)
+    dma("y", "d_fa", rows("inva"), A("lk0", 0, ROW))
+    for c in range(8):
+        spread("s", "d_v1", c, 1, after=[zeros])
+        spread("y", "d_v1", c + 8, 1)
+    dma("s", "d_b12", A("wb", M, R), hbm(T.b[:, M:R]))
+    iota(A("ci", 0, 16), [[1, 16]], 128, -1)
+    iota(A("ci", 16, 24), [[-16, 8]], 0, 1)
+    iota(A("ci", 24, 152), [[1, 128]], 0, -1)
+    numbers(0)
+    fill(A("sel", 0, 144), 0.0)
+    fill(A("pw", 0, PAD), 0.0)
+    fill(A("valb", 0, PAD), 0.0)
+    fill(A("r3", 0, PAD), 0.0)
+    fill(A("r4", 0, PAD), 0.0)
+    ts(A("cj", 0, 16), A("ci", 0, 16), 15, ALU.bitwise_and)
+    ts(A("cj", 16, 24), A("ci", 16, 24), 4, ALU.arith_shift_right)
+    ts(A("idb", 0, 128), A("ci", 24, 152), 0.0, ALU.is_equal)
+    ts(A("idn", 0, 128), A("ci", 24, 152), 0.0, ALU.is_equal, -1.0, ALU.mult)
+    ts(A("idp", 0, 128), A("ci", 24, 152), 0.0, ALU.is_equal)
+    ts(A("eq", 0, 16), A("cj", 0, 16), 0.0, ALU.is_equal)
+    ts(A("sel", 15, 143, 16), A("cj", 16, 24), 0.0, ALU.is_equal)
+    fill(A("lk1", 0, M), 0.0)
+
+    copy(A("so", 0, 28), A("sli", 0, 28))
+    copy(A("x1", 0, GH), I(A("wb", 0, M), A("so", 0, 14)))
+    sent1 = exchange(1, "x1", "wb", R, False)
+    positions(176, 352, [lambda: ts(A("si", 0, 14), A("sli", 14, 28), 4, ALU.arith_shift_right),
+                         lambda: ts(A("si", 16, 30), A("sli", 14, 28), 15, ALU.bitwise_and),
+                         lambda: ts(A("so", 28, 42), A("sli", 14, 28), float(-M), ALU.add)])
+    for k in range(1, 5):
+        numbers(k)
+    steps = links("lk1", 28)
+    invert(0, steps)
+    if SHOWN_FIRST:
+        copy(A("so", 70, 84), A("si", 16, 30))
+        ts(A("pl", 0, 176), A("enti", 0, 176), 2, ALU.arith_shift_right)
+        ts(A("so", 42, 56), A("si", 0, 14), -44.0, ALU.add)
+        ts(A("so", 56, 70), A("si", 0, 14), -40.0, ALU.add)
+        copy(A("msk", 0, GH), I(A("eq", 0, 16), A("so", 70, 84)))
+        ts(A("pl", 176, 352), A("enti", 176, 352), 2, ALU.arith_shift_right)
+        for e in range(4):
+            odd = e % 2
+            tt(A("gm", GH * e, GH * e + GH), I(A("pl", 44 * e - 4 * odd, 44 * e + 44), A("so", 42 + 14 * odd, 56 + 14 * odd)),
+               A("msk", 0, GH), ALU.mult)
+        deal("accp", "gm")
+    else:
+        ts(A("pl", 0, 352), A("enti", 0, 352), 2, ALU.arith_shift_right)
+    positions(0, 176, [lambda: copy(A("plu", 0, 118), A("pl", 0, 118)), lambda: copy(A("plu", 118, 236), A("pl", 118, 236)),
+                       lambda: copy(A("plu", 236, 352), A("pl", 236, 352))])
+    if SHOWN_FIRST:
+        for e in range(4):
+            x = I(A("valb", V1 + M * e, V1 + M * e + M), A("so", 28, 42))
+            if e < VCV:
+                copy(A("vc", GH * e, GH * e + GH), x)
+            else:
+                act(A("vc", GH * e, GH * e + GH), x, ACT.Copy)
+        copy(A("bsh", 0, GH), I(A("wb", 0, 2 * M), A("so", 14, 28)))
+    for c in range(16):
+        spread("y", "d_v2", c, 2, after=[sent1])
+    dma("y", "d_fb", rows("invb"), A("lk0", 0, ROW))
+    invert(1, steps)
+
+    wbw = A("wb", 0, R + GH)
+    if SHOWN_FIRST:
+        copy(A("pcu", 0, 56), A("accp", 0, 56))
+        level(GH, wbw, lambda e: A("pcu", 14 * e, 14 * e + 14), lambda e: A("vc", GH * e, GH * e + GH),
+              [("ps", GH * e) for e in range(4)], "accs", ("bsh", 0), A("x2", 0, GH), -1)
+        exchange(2, "x2", "w", R + GH, False)
+    level(M, wbw, lambda e: A("plu", 44 * e, 44 * e + 44), lambda e: A("valb", V1 + M * e, V1 + M * e + M),
+          [("w", 2 * M)] + [("pr", M * e) for e in range(1, 4)], "acc1", ("wb", M), A("w", M, 2 * M), -1)
+    if not SHOWN_FIRST:
+        copy(A("x2", 0, GH), I(A("w", M, 2 * M), A("so", 28, 42)))
+        exchange(2, "x2", "w", R + GH, False)
+    if CONV == "v":
+        copy(A("w", 0, M), A("wb", 0, M))
+    else:
+        act(A("w", 0, M), A("wb", 0, M), ACT.Copy)
+    copy(A("w", R, R + GH), A("wb", R, R + GH))
+    invert(2, steps)
+    invert(3, steps)
+    dma("y", "d_e1", A("ext", 0, ROW), rows("inva"))
+    for k in range(4, 8):
+        if k > 4:
+            numbers(k)
+        invert(k, steps)
+
+    level(M, A("w", 0, R + 2 * GH), lambda e: A("plu", 176 + 44 * e, 220 + 44 * e), lambda e: A("valb", V2 + M * e, V2 + M * e + M),
+          [("pr", M * e) for e in range(4)], "acc2", ("wb", 2 * M), None, -1)
+
+    pack("accp", 146, 14, ["ext"])
+    pack("accr", 44, 44, ["ext"])
+    deal("accq", "lk1")
+    products(V2, "acc2")
+    ts(A("og", 0, 56), A("accp", 0, 56), 0.25, ALU.add)
+    slots(A("x3", 0, GH), A("pw", 0, V1), "og", 0, 14, None, between=[
+        lambda: ts(A("oo", 0, 88), A("accr", 0, 88), 0.25, ALU.add),
+        lambda: ts(A("oo", 88, 176), A("accr", 88, 176), 0.25, ALU.add)])
+    sent3 = exchange(3, "x3", "r3", PAD, True)
+    dma("y", "d_e0", A("exb", 0, ROW), rows("invb"))
+    act(A("zw", 0, M), A("acc2", 0, M), ACT.Copy, -1.0)
+    for step in links("lk0", 0):
+        step()
+    dma("y", "d_z2", hbm(T.z[:, 2 * M:R]), A("zw", 0, M), after=[sent3])
+    pack("accp", 132, 14, ["ext", "exb"])
+    pack("accr", 0, 44, ["ext", "exb"])
+    slots(A("zw", M, 2 * M), A("pw", 0, V1), "oo", 0, 44, A("w", M, 2 * M))
+    ts(A("og", 56, 112), A("accp", 0, 56), 0.25, ALU.add)
+    ts(A("lu", 0, 56), A("accq", 0, 56), 1.0 / 16, ALU.mult, 0.25, ALU.add)
+    own0 = [lambda: ts(A("oo", 176, 264), A("accr", 0, 88), 0.25, ALU.add),
+            lambda: ts(A("oo", 264, 352), A("accr", 88, 176), 0.25, ALU.add)]
+    if GHOST_DIRECT:
+        act(A("vg", 0, 4 * GH), I(A("valb", 0, V1 + K4), A("og", 56, 112)), ACT.Copy, -1.0)
+        ts(A("gk", 0, 56), A("accp", 0, 56), 1.0 / M, ALU.mult, (0.5 - PAD) / M - 0.5, ALU.add)
+        ts(A("gn", 0, 56), A("accp", 0, 56), V1 - 0.5, ALU.is_ge, float(M), ALU.mult)
+        chain("r3", 0, [lambda: ts(A("gn", 56, 112), A("gk", 0, 56), float(-M), ALU.mult, 0.25 - PAD, ALU.add),
+                        lambda: tt(A("gn", 0, 56), A("gn", 0, 56), A("accp", 0, 56), ALU.add),
+                        lambda: tt(A("gn", 112, 168), A("gn", 0, 56), A("gn", 56, 112), ALU.add),
+                        lambda: copy(A("xu", 0, 56), A("gn", 112, 168))] + own0)
+    else:
+        chain("r3", 0, own0)
+    last("r3", 0, ("zw", M), 0, M)
+    dma("y", "d_z1", hbm(T.z[:, M:2 * M]), A("zw", M, 2 * M))
+
+    act(A("acc1", 0, M), A("zw", M, 2 * M), ACT.Copy, -1.0)
+    if GHOST_DIRECT:
+        level(GH, A("zw", 0, 2 * M), lambda e: A("xu", 14 * e, 14 * e + 14), lambda e: A("vg", GH * e, GH * e + GH),
+              [("ps", GH * e) for e in range(4)], "accs", None, A("x4", 0, GH), 1)
+        exchange(4, "x4", "r4", PAD, True)
+    deal("accq", "lk0")
+    products(V1, "acc1")
+    pww = A("pw", 0, V1 + K4)
+    if not GHOST_DIRECT:
+        slots(A("x4", 0, GH), pww, "og", 56, 14, None)
+        exchange(4, "x4", "r4", PAD, True)
+    lu0 = [lambda: ts(A("lu", 56, 112), A("accq", 0, 56), 1.0 / 16, ALU.mult, 0.25, ALU.add)]
+    if SHARE:
+        part = SHARE - M
+        for lo, hi in banks(M):
+            mm(A("acc2", lo, hi), A("idb", 0, 128), A("wb", lo, hi), True, False)
+        pieces = [(2, lo, min(lo + 256, part)) for lo in range(0, part, 256)] + [(3, 0, 256), (3, 256, 512), (3, 512, M)]
+        for s, lo, hi in pieces:
+            act(A("pr", M * s + lo, M * s + hi), I(pww, A("oo", 176 + 44 * s + lo // 16, 176 + 44 * s + hi // 16)), ACT.Copy)
+            mm(A("acc2", lo, hi), A("idp", 0, 128), A("pr", M * s + lo, M * s + hi), False, s == 3 and hi >= 512)
+        slots(A("z0", 0, M), pww, "oo", 176, 44, None, 2, between=lu0)
+        if part < M:
+            slot(A("z0", part, M), pww, A("oo", 264 + part // 16, 308), A("z0", part, M))
+        tt(A("z0", 0, M), A("z0", 0, M), A("acc2", 0, M), ALU.add)
+    else:
+        slots(A("z0", 0, M), pww, "oo", 176, 44, A("w", 0, M), between=lu0)
+    chain("r4", 56)
+    H = M // 2
+    last("r4", 56, ("z0", 0), 0, H)
+    dma("y", "d_z0", hbm(T.z[:, 0:H]), A("z0", 0, H))
+    last("r4", 56, ("z0", 0), H, M)
+    dma("s", "d_z0b", hbm(T.z[:, H:M]), A("z0", H, M))
+    emit(g, T, ops)

@@ -7,75 +7,34 @@ K4 = 4 * M
 PAD = 32
 V2, V1 = PAD, PAD + K4
 ROW = 640
-NPE = 2
-SHOWN_FIRST = True
-GHOST_DIRECT = True
-TWO_CALLS = True
-VCV = 4
-CONV = "s"
-SHARE = M
+THIRD = 512
+SHARE = 256
 
-SCRATCH = {
-    "wb": ("sbuf", [128, R + GH], "bfloat16"),
-    "w": ("sbuf", [128, R + 2 * GH], "float32"),
-    "valb": ("sbuf", [128, PAD + 2 * K4], "bfloat16"),
-    "pw": ("sbuf", [128, PAD + 2 * K4], "float32"),
-    "num": ("sbuf", [128, 2 * K4], "float32"),
-    "inva": ("sbuf", [128, 16 * ROW], "float32"),
-    "invb": ("sbuf", [128, 16 * ROW], "float32"),
-    "ext": ("sbuf", [128, ROW], "float32"),
-    "exb": ("sbuf", [128, ROW], "float32"),
-    "lk1": ("sbuf", [128, M + 6 * S], "float32"),
-    "lk0": ("sbuf", [128, M + 6 * S], "float32"),
-    "lu": ("sbuf", [128, 112], "uint16"),
-    "enti": ("sbuf", [128, 352], "int32"),
-    "pl": ("sbuf", [128, 352], "int32"),
-    "plu": ("sbuf", [128, 352], "uint16"),
-    "qa": ("sbuf", [128, 352], "int32"),
-    "qb": ("sbuf", [128, 352], "float32"),
-    "qu": ("sbuf", [128, 352], "uint16"),
-    "sli": ("sbuf", [128, 28], "int32"),
-    "si": ("sbuf", [128, 32], "int32"),
-    "so": ("sbuf", [128, 84], "uint16"),
-    "ci": ("sbuf", [128, 152], "int32"),
-    "cj": ("sbuf", [128, 24], "int32"),
-    "eq": ("sbuf", [128, 16], "float32"),
-    "sel": ("sbuf", [128, 144], "float32"),
-    "idb": ("sbuf", [128, 128], "bfloat16"),
-    "idn": ("sbuf", [128, 128], "float32"),
-    "idp": ("sbuf", [128, 128], "float32"),
-    "msk": ("sbuf", [128, GH], "float32"),
-    "gm": ("sbuf", [128, 4 * GH], "float32"),
-    "pcu": ("sbuf", [128, 56], "uint16"),
-    "vc": ("sbuf", [128, 4 * GH], "bfloat16"),
-    "vg": ("sbuf", [128, 4 * GH], "bfloat16"),
-    "bsh": ("sbuf", [128, GH], "bfloat16"),
-    "pr": ("sbuf", [128, K4], "float32"),
-    "ps": ("sbuf", [128, 4 * GH], "float32"),
-    "x1": ("sbuf", [128, GH], "bfloat16"),
-    "x2": ("sbuf", [128, GH], "float32"),
-    "x3": ("sbuf", [128, GH], "float32"),
-    "x4": ("sbuf", [128, GH], "float32"),
-    "r3": ("sbuf", [128, PAD + GH], "float32"),
-    "r4": ("sbuf", [128, PAD + GH], "float32"),
-    "og": ("sbuf", [128, 112], "uint16"),
-    "oo": ("sbuf", [128, 352], "uint16"),
-    "gn": ("sbuf", [128, 168], "float32"),
-    "gk": ("sbuf", [128, 56], "int32"),
-    "xu": ("sbuf", [128, 56], "uint16"),
-    "zw": ("sbuf", [128, 2 * M], "float32"),
-    "z0": ("sbuf", [128, M], "float32"),
-    "acc1": ("psum", [128, 1024], "float32"),
-    "acc2": ("psum", [128, 1024], "float32"),
-    "accs": ("psum", [128, 512], "float32"),
-    "accp": ("psum", [128, 512], "float32"),
-    "accq": ("psum", [128, 512], "float32"),
-    "accr": ("psum", [128, 512], "float32"),
+F, B, J, U = "float32", "bfloat16", "int32", "uint16"
+SBUF = {
+    "wb": (R + GH, B),
+    "w": (R + 2 * GH, F),
+    "valb": (PAD + 2 * K4, B), "pw": (PAD + 2 * K4, F), "num": (2 * K4, F),
+    "inva": (16 * ROW, F),
+    "invb": (16 * ROW, F),
+    "ext": (ROW, F), "exb": (ROW, F),
+    "lk1": (M + 6 * S, F),
+    "lk0": (M + 6 * S, F),
+    "lu": (112, U), "enti": (352, J), "pl": (352, J), "plu": (352, U), "qa": (352, J), "qb": (352, F), "qu": (352, U),
+    "sli": (28, J), "si": (32, J), "so": (84, U), "ci": (152, J), "cj": (24, J), "eq": (16, F), "sel": (144, F),
+    "idb": (128, B), "idn": (128, F), "idp": (128, F), "msk": (GH, F), "gm": (4 * GH, F), "pcu": (56, U),
+    "vc": (4 * GH, B), "vg": (4 * GH, B), "bsh": (GH, B), "pr": (K4, F), "ps": (4 * GH, F),
+    "x1": (GH, B), "x2": (GH, F), "x3": (GH, F), "x4": (GH, F), "r3": (PAD + GH, F), "r4": (PAD + GH, F),
+    "og": (112, U), "oo": (352, U), "gn": (168, F), "gk": (56, J), "xu": (56, U),
+    "zw": (2 * M, F),
+    "z0": (M, F),
 }
+PSUM = {"acc1": 1024, "acc2": 1024, "accs": 512, "accp": 512, "accq": 512, "accr": 512}
+SCRATCH = {k: ("sbuf", [128, n], t) for k, (n, t) in SBUF.items()}
+SCRATCH.update({k: ("psum", [128, n], F) for k, n in PSUM.items()})
 DMA_SEMS = ["d_sl", "d_b0", "d_ent", "d_fa", "d_fb", "d_v1", "d_v2", "d_b12", "d_e1", "d_e0", "d_z2", "d_z1", "d_z0", "d_z0b"]
 OWN_SEMS = ["s_v", "s_s", "s_t", "s_g"]
 SEMAPHORES = OWN_SEMS + ["arr%d" % k for k in range(1, 5)] + ["snt%d%s" % (k, c) for k in range(1, 5) for c in "ab"] + DMA_SEMS
-PSUM = ("acc1", "acc2", "accs", "accp", "accq", "accr")
 ALU, ACT = AluOpType, ActivationFunctionType
 
 
@@ -91,8 +50,6 @@ def calls_of(T, topo, r, back):
 
     def mask(es):
         return sum(1 << e for e in es)
-    if not TWO_CALLS:
-        return [[(d, q, mask([eo[i]])) for i, (d, q) in enumerate(off)] + [(on[0][0], on[0][1], mask(ei[:1]))]]
     a, b = len(eo) // 4, len(eo) // 2
     first = [(d, q, mask(eo[a * i:a * i + a])) for i, (d, q) in enumerate(off[:4])] + [(on[0][0], on[0][1], mask(ei[:2]))]
     second = [(d, q, mask(eo[b * i:b * i + b])) for i, (d, q) in enumerate(off[4:])]
@@ -129,7 +86,7 @@ def emit(g, T, ops):
                     if b1 != b2:
                         continue
                     if b1 in PSUM and o["q"] != p["q"]:
-                        hit = True
+                        hit = hit or (l1 // 512 <= (h2 - 1) // 512 and l2 // 512 <= (h1 - 1) // 512)
                     elif l1 < h2 and l2 < h1 and (w1 or w2) and not (b1 in PSUM and o["q"] == "t"):
                         hit = True
             if hit:
@@ -232,23 +189,28 @@ def rank_program(g, core, T, topo):
     def sub(x, lo, hi):
         return A(x[0], x[1] + lo, x[1] + hi)
 
-    def level(n, win, off, fac, prod, acc, base, out, sign):
+    def level(n, win, off, fac, prod, acc, base, out, sign, gap=None):
         ident = A("idn" if sign < 0 else "idp", 0, 128)
         op = ALU.subtract if sign < 0 else ALU.add
         if base is not None:
             for lo, hi in banks(n):
                 mm(A(acc, lo, hi), A("idb", 0, 128), sub(base, lo, hi), True, False)
+        third = THIRD if n > 512 else 0
         for e in range(4):
-            tt(sub(prod[e], 0, n), I(win, off(e)), fac(e), ALU.mult)
-            if e < NPE:
-                for lo, hi in banks(n):
-                    mm(A(acc, lo, hi), ident, sub(prod[e], lo, hi), base is None and e == 0, e == NPE - 1)
-        for e in range(NPE, 3):
-            tt(A(acc, 0, n), A(acc, 0, n), sub(prod[e], 0, n), op)
-        if out is None:
-            tt(A(acc, 0, n), sub(prod[3], 0, n), A(acc, 0, n), ALU.subtract)
-        else:
-            tt(out, A(acc, 0, n), sub(prod[3], 0, n), op)
+            for lo, hi in ((0, 256), (256, n)) if e == 0 and n > 512 else ((0, n),):
+                tt(sub(prod[e], lo, hi), I(win, sub(off(e), lo // 16, hi // 16)), sub(fac(e), lo, hi), ALU.mult)
+                for a, b in banks(n):
+                    a, b = max(a, lo), min(b, hi, third if e == 2 else n)
+                    if e < 3 and a < b:
+                        mm(A(acc, a, b), ident, sub(prod[e], a, b), base is None and e == 0, e == 2 or (e == 1 and a >= third))
+        tt(A(acc, third, n), A(acc, third, n), sub(prod[2], third, n), op)
+        if gap:
+            gap()
+        for lo, hi in reversed(banks(n)):
+            if out is None:
+                tt(A(acc, lo, hi), sub(prod[3], lo, hi), A(acc, lo, hi), ALU.subtract)
+            else:
+                tt(sub(out, lo, hi), A(acc, lo, hi), sub(prod[3], lo, hi), op)
 
     def positions(lo, hi, between):
         ts(A("qa", lo, hi), A("enti", lo, hi), 63, ALU.bitwise_and)
@@ -322,7 +284,7 @@ def rank_program(g, core, T, topo):
     for c in range(8):
         spread("s", "d_v1", c, 1, after=[zeros])
         spread("y", "d_v1", c + 8, 1)
-    dma("s", "d_b12", A("wb", M, R), hbm(T.b[:, M:R]))
+    dma("y", "d_b12", A("wb", M, R), hbm(T.b[:, M:R]))
     iota(A("ci", 0, 16), [[1, 16]], 128, -1)
     iota(A("ci", 16, 24), [[-16, 8]], 0, 1)
     iota(A("ci", 24, 152), [[1, 128]], 0, -1)
@@ -339,72 +301,58 @@ def rank_program(g, core, T, topo):
     ts(A("idp", 0, 128), A("ci", 24, 152), 0.0, ALU.is_equal)
     ts(A("eq", 0, 16), A("cj", 0, 16), 0.0, ALU.is_equal)
     ts(A("sel", 15, 143, 16), A("cj", 16, 24), 0.0, ALU.is_equal)
-    fill(A("lk1", 0, M), 0.0)
+    act(A("lk1", 0, M), A("lk0", 0, M), ACT.Copy)
+    act(A("w", 0, M), A("wb", 0, M), ACT.Copy)
 
     copy(A("so", 0, 28), A("sli", 0, 28))
+    ts(A("so", 28, 42), A("sli", 14, 28), float(-M), ALU.add)
     copy(A("x1", 0, GH), I(A("wb", 0, M), A("so", 0, 14)))
     sent1 = exchange(1, "x1", "wb", R, False)
+    steps = links("lk1", 28)
+    steps.pop(0)()
     positions(176, 352, [lambda: ts(A("si", 0, 14), A("sli", 14, 28), 4, ALU.arith_shift_right),
                          lambda: ts(A("si", 16, 30), A("sli", 14, 28), 15, ALU.bitwise_and),
-                         lambda: ts(A("so", 28, 42), A("sli", 14, 28), float(-M), ALU.add)])
+                         lambda: copy(A("so", 70, 84), A("si", 16, 30))])
     for k in range(1, 5):
         numbers(k)
-    steps = links("lk1", 28)
     invert(0, steps)
-    if SHOWN_FIRST:
-        copy(A("so", 70, 84), A("si", 16, 30))
-        ts(A("pl", 0, 176), A("enti", 0, 176), 2, ALU.arith_shift_right)
-        ts(A("so", 42, 56), A("si", 0, 14), -44.0, ALU.add)
-        ts(A("so", 56, 70), A("si", 0, 14), -40.0, ALU.add)
-        copy(A("msk", 0, GH), I(A("eq", 0, 16), A("so", 70, 84)))
-        ts(A("pl", 176, 352), A("enti", 176, 352), 2, ALU.arith_shift_right)
-        for e in range(4):
-            odd = e % 2
-            tt(A("gm", GH * e, GH * e + GH), I(A("pl", 44 * e - 4 * odd, 44 * e + 44), A("so", 42 + 14 * odd, 56 + 14 * odd)),
-               A("msk", 0, GH), ALU.mult)
-        deal("accp", "gm")
-    else:
-        ts(A("pl", 0, 352), A("enti", 0, 352), 2, ALU.arith_shift_right)
+    ts(A("pl", 0, 176), A("enti", 0, 176), 2, ALU.arith_shift_right)
+    ts(A("so", 42, 56), A("si", 0, 14), -44.0, ALU.add)
+    ts(A("so", 56, 70), A("si", 0, 14), -40.0, ALU.add)
+    copy(A("msk", 0, GH), I(A("eq", 0, 16), A("so", 70, 84)))
+    ts(A("pl", 176, 352), A("enti", 176, 352), 2, ALU.arith_shift_right)
+    for e in range(4):
+        odd = e % 2
+        tt(A("gm", GH * e, GH * e + GH), I(A("pl", 44 * e - 4 * odd, 44 * e + 44), A("so", 42 + 14 * odd, 56 + 14 * odd)),
+           A("msk", 0, GH), ALU.mult)
+    deal("accp", "gm")
     positions(0, 176, [lambda: copy(A("plu", 0, 118), A("pl", 0, 118)), lambda: copy(A("plu", 118, 236), A("pl", 118, 236)),
                        lambda: copy(A("plu", 236, 352), A("pl", 236, 352))])
-    if SHOWN_FIRST:
-        for e in range(4):
-            x = I(A("valb", V1 + M * e, V1 + M * e + M), A("so", 28, 42))
-            if e < VCV:
-                copy(A("vc", GH * e, GH * e + GH), x)
-            else:
-                act(A("vc", GH * e, GH * e + GH), x, ACT.Copy)
-        copy(A("bsh", 0, GH), I(A("wb", 0, 2 * M), A("so", 14, 28)))
+    for e in range(4):
+        copy(A("vc", GH * e, GH * e + GH), I(A("valb", V1 + M * e, V1 + M * e + M), A("so", 28, 42)))
+    copy(A("bsh", 0, GH), I(A("wb", 0, 2 * M), A("so", 14, 28)))
     for c in range(16):
         spread("y", "d_v2", c, 2, after=[sent1])
     dma("y", "d_fb", rows("invb"), A("lk0", 0, ROW))
     invert(1, steps)
 
     wbw = A("wb", 0, R + GH)
-    if SHOWN_FIRST:
-        copy(A("pcu", 0, 56), A("accp", 0, 56))
-        level(GH, wbw, lambda e: A("pcu", 14 * e, 14 * e + 14), lambda e: A("vc", GH * e, GH * e + GH),
-              [("ps", GH * e) for e in range(4)], "accs", ("bsh", 0), A("x2", 0, GH), -1)
-        exchange(2, "x2", "w", R + GH, False)
-    level(M, wbw, lambda e: A("plu", 44 * e, 44 * e + 44), lambda e: A("valb", V1 + M * e, V1 + M * e + M),
-          [("w", 2 * M)] + [("pr", M * e) for e in range(1, 4)], "acc1", ("wb", M), A("w", M, 2 * M), -1)
-    if not SHOWN_FIRST:
-        copy(A("x2", 0, GH), I(A("w", M, 2 * M), A("so", 28, 42)))
-        exchange(2, "x2", "w", R + GH, False)
-    if CONV == "v":
-        copy(A("w", 0, M), A("wb", 0, M))
-    else:
-        act(A("w", 0, M), A("wb", 0, M), ACT.Copy)
-    copy(A("w", R, R + GH), A("wb", R, R + GH))
+    copy(A("pcu", 0, 56), A("accp", 0, 56))
+    level(GH, wbw, lambda e: ("pcu", 14 * e), lambda e: ("vc", GH * e),
+          [("ps", GH * e) for e in range(4)], "accs", ("bsh", 0), ("x2", 0), -1)
+    sent2 = exchange(2, "x2", "w", R + GH, False)
+    level(M, wbw, lambda e: ("plu", 44 * e), lambda e: ("valb", V1 + M * e),
+          [("w", 2 * M)] + [("pr", M * e) for e in range(1, 4)], "acc1", ("wb", M), ("w", M), -1,
+          lambda: copy(A("w", R, R + GH), A("wb", R, R + GH)))
     invert(2, steps)
     invert(3, steps)
-    dma("y", "d_e1", A("ext", 0, ROW), rows("inva"))
+    dma("y", "d_e1", A("ext", 0, ROW), rows("inva"), after=[sent2])
     for k in range(4, 8):
         if k > 4:
             numbers(k)
         invert(k, steps)
 
-    level(M, A("w", 0, R + 2 * GH), lambda e: A("plu", 176 + 44 * e, 220 + 44 * e), lambda e: A("valb", V2 + M * e, V2 + M * e + M),
+    level(M, A("w", 0, R + 2 * GH), lambda e: ("plu", 176 + 44 * e), lambda e: ("valb", V2 + M * e),
           [("pr", M * e) for e in range(4)], "acc2", ("wb", 2 * M), None, -1)
 
     pack("accp", 146, 14, ["ext"])
@@ -423,52 +371,40 @@ def rank_program(g, core, T, topo):
     dma("y", "d_z2", hbm(T.z[:, 2 * M:R]), A("zw", 0, M), after=[sent3])
     pack("accp", 132, 14, ["ext", "exb"])
     pack("accr", 0, 44, ["ext", "exb"])
-    slots(A("zw", M, 2 * M), A("pw", 0, V1), "oo", 0, 44, A("w", M, 2 * M))
+    slots(A("zw", M, 2 * M), A("pw", 0, V1), "oo", 0, 44, A("w", M, 2 * M), between=[
+        lambda: None, lambda: None, lambda: ts(A("lu", 0, 56), A("accq", 0, 56), 1.0 / 16, ALU.mult, 0.25, ALU.add)])
     ts(A("og", 56, 112), A("accp", 0, 56), 0.25, ALU.add)
-    ts(A("lu", 0, 56), A("accq", 0, 56), 1.0 / 16, ALU.mult, 0.25, ALU.add)
-    own0 = [lambda: ts(A("oo", 176, 264), A("accr", 0, 88), 0.25, ALU.add),
-            lambda: ts(A("oo", 264, 352), A("accr", 88, 176), 0.25, ALU.add)]
-    if GHOST_DIRECT:
-        act(A("vg", 0, 4 * GH), I(A("valb", 0, V1 + K4), A("og", 56, 112)), ACT.Copy, -1.0)
-        ts(A("gk", 0, 56), A("accp", 0, 56), 1.0 / M, ALU.mult, (0.5 - PAD) / M - 0.5, ALU.add)
-        ts(A("gn", 0, 56), A("accp", 0, 56), V1 - 0.5, ALU.is_ge, float(M), ALU.mult)
-        chain("r3", 0, [lambda: ts(A("gn", 56, 112), A("gk", 0, 56), float(-M), ALU.mult, 0.25 - PAD, ALU.add),
-                        lambda: tt(A("gn", 0, 56), A("gn", 0, 56), A("accp", 0, 56), ALU.add),
-                        lambda: tt(A("gn", 112, 168), A("gn", 0, 56), A("gn", 56, 112), ALU.add),
-                        lambda: copy(A("xu", 0, 56), A("gn", 112, 168))] + own0)
-    else:
-        chain("r3", 0, own0)
+    act(A("vg", 0, 4 * GH), I(A("valb", 0, V1 + K4), A("og", 56, 112)), ACT.Copy, -1.0)
+    ts(A("gk", 0, 56), A("accp", 0, 56), 1.0 / M, ALU.mult, (0.5 - PAD) / M - 0.5, ALU.add)
+    ts(A("gn", 0, 56), A("accp", 0, 56), V1 - 0.5, ALU.is_ge, float(M), ALU.mult)
+    chain("r3", 0, [lambda: ts(A("gn", 56, 112), A("gk", 0, 56), float(-M), ALU.mult, 0.25 - PAD, ALU.add),
+                    lambda: tt(A("gn", 0, 56), A("gn", 0, 56), A("accp", 0, 56), ALU.add),
+                    lambda: tt(A("gn", 112, 168), A("gn", 0, 56), A("gn", 56, 112), ALU.add),
+                    lambda: copy(A("xu", 0, 56), A("gn", 112, 168)),
+                    lambda: ts(A("oo", 176, 264), A("accr", 0, 88), 0.25, ALU.add),
+                    lambda: ts(A("oo", 264, 352), A("accr", 88, 176), 0.25, ALU.add)])
     last("r3", 0, ("zw", M), 0, M)
-    dma("y", "d_z1", hbm(T.z[:, M:2 * M]), A("zw", M, 2 * M))
 
     act(A("acc1", 0, M), A("zw", M, 2 * M), ACT.Copy, -1.0)
-    if GHOST_DIRECT:
-        level(GH, A("zw", 0, 2 * M), lambda e: A("xu", 14 * e, 14 * e + 14), lambda e: A("vg", GH * e, GH * e + GH),
-              [("ps", GH * e) for e in range(4)], "accs", None, A("x4", 0, GH), 1)
-        exchange(4, "x4", "r4", PAD, True)
+    level(GH, A("zw", 0, 2 * M), lambda e: ("xu", 14 * e), lambda e: ("vg", GH * e),
+          [("ps", GH * e) for e in range(4)], "accs", None, ("x4", 0), 1)
+    sent4 = exchange(4, "x4", "r4", PAD, True)
+    dma("y", "d_z1", hbm(T.z[:, M:2 * M]), A("zw", M, 2 * M), after=[sent4])
     deal("accq", "lk0")
     products(V1, "acc1")
     pww = A("pw", 0, V1 + K4)
-    if not GHOST_DIRECT:
-        slots(A("x4", 0, GH), pww, "og", 56, 14, None)
-        exchange(4, "x4", "r4", PAD, True)
-    lu0 = [lambda: ts(A("lu", 56, 112), A("accq", 0, 56), 1.0 / 16, ALU.mult, 0.25, ALU.add)]
-    if SHARE:
-        part = SHARE - M
-        for lo, hi in banks(M):
-            mm(A("acc2", lo, hi), A("idb", 0, 128), A("wb", lo, hi), True, False)
-        pieces = [(2, lo, min(lo + 256, part)) for lo in range(0, part, 256)] + [(3, 0, 256), (3, 256, 512), (3, 512, M)]
-        for s, lo, hi in pieces:
-            act(A("pr", M * s + lo, M * s + hi), I(pww, A("oo", 176 + 44 * s + lo // 16, 176 + 44 * s + hi // 16)), ACT.Copy)
-            mm(A("acc2", lo, hi), A("idp", 0, 128), A("pr", M * s + lo, M * s + hi), False, s == 3 and hi >= 512)
-        slots(A("z0", 0, M), pww, "oo", 176, 44, None, 2, between=lu0)
-        if part < M:
-            slot(A("z0", part, M), pww, A("oo", 264 + part // 16, 308), A("z0", part, M))
-        tt(A("z0", 0, M), A("z0", 0, M), A("acc2", 0, M), ALU.add)
-    else:
-        slots(A("z0", 0, M), pww, "oo", 176, 44, A("w", 0, M), between=lu0)
-    chain("r4", 56)
-    H = M // 2
+    for lo, hi in banks(M):
+        mm(A("acc2", lo, hi), A("idb", 0, 128), A("wb", lo, hi), True, False)
+    for s, lo, hi in [(3, 512, M), (2, 0, SHARE), (3, 0, 256), (3, 256, 512)]:
+        act(A("pr", M * s + lo, M * s + hi), I(pww, A("oo", 176 + 44 * s + lo // 16, 176 + 44 * s + hi // 16)), ACT.Copy)
+        mm(A("acc2", lo, hi), A("idp", 0, 128), A("pr", M * s + lo, M * s + hi), False, s == 3 and hi >= 512)
+    slots(A("z0", 0, M), pww, "oo", 176, 44, None, 2,
+          between=[lambda: ts(A("lu", 56, 112), A("accq", 0, 56), 1.0 / 16, ALU.mult, 0.25, ALU.add)])
+    slot(A("z0", SHARE, M), pww, A("oo", 264 + SHARE // 16, 308), A("z0", SHARE, M))
+    tt(A("z0", 0, 256), A("z0", 0, 256), A("acc2", 0, 256), ALU.add)
+    chain("r4", 56, [lambda lo=lo: tt(A("z0", lo, lo + 112), A("z0", lo, lo + 112), A("acc2", lo, lo + 112), ALU.add)
+                     for lo in range(256, M, 112)])
+    H = 448
     last("r4", 56, ("z0", 0), 0, H)
     dma("y", "d_z0", hbm(T.z[:, 0:H]), A("z0", 0, H))
     last("r4", 56, ("z0", 0), H, M)

from concourse.bass import DstId, RemoteDMATransfer
from concourse.mybir import AluOpType, ActivationFunctionType

N, M, S = 8, 704, 32
R, GH = 3 * M, 7 * S
K4 = 4 * M
PAD = 32
V2, V1 = PAD, PAD + K4
ROW = 640
THIRD = 512
SHARE = 256

F, B, J, U = "float32", "bfloat16", "int32", "uint16"
SBUF = {
    "wb": (R + GH, B),
    "w": (R + 2 * GH, F),
    "valb": (PAD + 2 * K4, B), "pw": (PAD + 2 * K4, F), "num": (2 * K4, F),
    "inva": (16 * ROW, F),
    "invb": (16 * ROW, F),
    "ext": (ROW, F), "exb": (ROW, F),
    "lk1": (M + 6 * S, F),
    "lk0": (M + 6 * S, F),
    "lu": (112, U), "enti": (352, J), "pl": (352, J), "plu": (352, U), "qa": (352, J), "qb": (352, F), "qu": (352, U),
    "sli": (28, J), "si": (32, J), "so": (84, U), "ci": (152, J), "cj": (24, J), "eq": (16, F), "sel": (144, F),
    "idb": (128, B), "idn": (128, F), "idp": (128, F), "msk": (GH, F), "gm": (4 * GH, F), "pcu": (56, U),
    "vc": (4 * GH, B), "vg": (4 * GH, B), "bsh": (GH, B), "pr": (K4, F), "ps": (4 * GH, F),
    "x1": (GH, B), "x2": (GH, F), "x3": (GH, F), "x4": (GH, F), "r3": (PAD + GH, F), "r4": (PAD + GH, F),
    "og": (112, U), "oo": (352, U), "gn": (168, F), "gk": (56, J), "xu": (56, U),
    "zw": (2 * M, F),
    "z0": (M, F),
}
PSUM = {"acc1": 1024, "acc2": 1024, "accs": 512, "accp": 512, "accq": 512, "accr": 512}
SCRATCH = {k: ("sbuf", [128, n], t) for k, (n, t) in SBUF.items()}
SCRATCH.update({k: ("psum", [128, n], F) for k, n in PSUM.items()})
DMA_SEMS = ["d_sl", "d_b0", "d_ent", "d_fa", "d_fb", "d_v1", "d_v2", "d_b12", "d_e1", "d_e0", "d_z2", "d_z1", "d_z0", "d_z0b"]
OWN_SEMS = ["s_v", "s_s", "s_t", "s_g"]
SEMAPHORES = OWN_SEMS + ["arr%d" % k for k in range(1, 5)] + ["snt%d%s" % (k, c) for k in range(1, 5) for c in "ab"] + DMA_SEMS
ALU, ACT = AluOpType, ActivationFunctionType


def calls_of(T, topo, r, back):
    src = T.cores[r]
    on, off = [], []
    for d in range(N - 1):
        q = (r - 1 - d) % N if back else (r + 1 + d) % N
        (on if T.cores[q] in topo.cores_of(src) else off).append((d, q))
    off.sort(key=lambda x: (topo.mates(src, T.cores[x[1]]), topo.same_plane(src, T.cores[x[1]])))
    eo = topo.engines(src, T.cores[off[0][1]])
    ei = [e for e in topo.engines(src, T.cores[on[0][1]]) if e not in eo]

    def mask(es):
        return sum(1 << e for e in es)
    a, b = len(eo) // 4, len(eo) // 2
    first = [(d, q, mask(eo[a * i:a * i + a])) for i, (d, q) in enumerate(off[:4])] + [(on[0][0], on[0][1], mask(ei[:2]))]
    second = [(d, q, mask(eo[b * i:b * i + b])) for i, (d, q) in enumerate(off[4:])]
    return [first, second]


def bits(m):
    return bin(m).count("1")


def emit(g, T, ops):
    queues = {"v": g.vector, "s": g.scalar, "t": g.tensor, "g": g, "y": g.sync}
    total, count = {}, {}
    for o in ops:
        if o["sem"] not in OWN_SEMS:
            total[o["sem"]] = total.get(o["sem"], 0) + o["inc"]
    known = {q: {} for q in queues}
    for i, o in enumerate(ops):
        own = o["sem"] not in total
        if own:
            count[o["sem"]] = count.get(o["sem"], 0) + 1
        o["tok"] = count[o["sem"]] if own else total[o["sem"]]
        if o["q"] is None:
            o["clock"] = {}
            continue
        kn = known[o["q"]]
        deps = list(o["after"])
        for p in ops[:i]:
            if p["sem"] == o["sem"] and not own:
                continue
            hit = False
            for (b1, l1, h1, w1) in o["acc"]:
                for (b2, l2, h2, w2) in p["acc"]:
                    if b1 != b2:
                        continue
                    if b1 in PSUM and o["q"] != p["q"]:
                        hit = hit or (l1 // 512 <= (h2 - 1) // 512 and l2 // 512 <= (h1 - 1) // 512)
                    elif l1 < h2 and l2 < h1 and (w1 or w2) and not (b1 in PSUM and o["q"] == "t"):
                        hit = True
            if hit:
                deps.append(p)
        for p in reversed(deps):
            if kn.get(p["sem"], 0) < p["tok"]:
                queues[o["q"]].wait_ge(T.sem[p["sem"]], p["tok"])
                kn[p["sem"]] = p["tok"]
                for s, c in p["clock"].items():
                    kn[s] = max(kn.get(s, 0), c)
        o["clock"] = dict(kn)
        ins = o["fn"](queues[o["q"]])
        if o["then"]:
            ins.then_inc(T.sem[o["sem"]], o["inc"])
    for s, c in list(count.items()) + list(total.items()):
        if max(known[q].get(s, 0) for q in known) < c:
            g.wait_ge(T.sem[s], c)


def rank_program(g, core, T, topo):
    rank = T.rank_of(core)
    if rank is None:
        return
    ops = []

    def A(name, lo, hi, step=1):
        return (T[name][:, lo:hi] if step == 1 else T[name][:, lo:hi:step], [(name, lo, hi)])

    def I(win, off):
        return (win[0].indirect(off[0]), win[1], off[1])

    def rec(q, sem, inc, fn, outs, ins, then=True, after=()):
        acc = []
        for x in outs:
            acc += [r + (True,) for r in x[1]] + ([r + (False,) for r in x[2]] if len(x) > 2 else [])
        for x in ins:
            acc += [r + (False,) for r in x[1]] + ([r + (False,) for r in x[2]] if len(x) > 2 else [])
        o = {"q": q, "sem": sem, "inc": inc, "fn": fn, "acc": acc, "then": then, "after": list(after)}
        ops.append(o)
        return o

    def copy(out, a):
        return rec("v", "s_v", 1, lambda e: e.tensor_copy(out[0], a[0]), [out], [a])

    def tt(out, a, b, op):
        return rec("v", "s_v", 1, lambda e: e.tensor_tensor(out[0], a[0], b[0], op), [out], [a, b])

    def ts(out, a, s1, op0, s2=None, op1=None):
        if s2 is None:
            return rec("v", "s_v", 1, lambda e: e.tensor_scalar(out[0], a[0], s1, None, op0), [out], [a])
        return rec("v", "s_v", 1, lambda e: e.tensor_scalar(out[0], a[0], s1, s2, op0, op1), [out], [a])

    def fill(out, c):
        return rec("v", "s_v", 1, lambda e: e.memset(out[0], c), [out], [])

    def act(out, a, func, scale=None):
        if scale is None:
            return rec("s", "s_s", 1, lambda e: e.activation(out[0], a[0], func), [out], [a])
        return rec("s", "s_s", 1, lambda e: e.activation(out[0], a[0], func, scale=scale), [out], [a])

    def mm(out, lhs, rhs, start, stop):
        return rec("t", "s_t", 1, lambda e: e.matmul(out[0], lhs[0], rhs[0], start, stop), [out], [lhs, rhs])

    def iota(out, pattern, base, cm, flt=False):
        if flt:
            return rec("g", "s_g", 1, lambda e: e.iota(out[0], pattern, base, cm, allow_small_or_imprecise_dtypes=True), [out], [])
        return rec("g", "s_g", 1, lambda e: e.iota(out[0], pattern, base, cm), [out], [])

    def dma(q, sem, out, a, after=()):
        return rec(q, sem, 16, lambda e: e.dma_start(out[0], a[0]), [out], [a], after=after)

    def hbm(ap):
        return (ap, [])

    def exchange(k, src, dst, col, back):
        sent = []
        for call, tag in zip(calls_of(T, topo, rank, back), "ab"):
            trs = []
            for (d, q, m) in call:
                rid, pid = topo.addr(T.cores[q], core)
                trs.append(RemoteDMATransfer(dst_ids=[DstId(rid=rid, pnc=pid)], dma_engine_mask=m, remote_sem=T.sem["arr%d" % k],
                                             src=T[src][:, S * d:S * d + S], dst=T[dst][:, col + S * d:col + S * d + S]))
            name = "snt%d%s" % (k, tag)
            sent.append(rec("g", name, sum(bits(m) for (d, q, m) in call),
                            lambda e, trs=trs, name=name: e.remote_dma_fused(trs, local_sem=T.sem[name]), [], [A(src, 0, GH)], then=False))
        n = sum(bits(m) for r in range(N) for call in calls_of(T, topo, r, back) for (d, q, m) in call if q == rank)
        rec(None, "arr%d" % k, n, None, [A(dst, col, col + GH)], [])
        return sent[0]

    def spread(q, sem, c, lvl, after=()):
        col = V1 if lvl == 1 else V2
        return dma(q, sem, (T.valb[c:128:16, col:col + K4], [("valb", col, col + K4)]), hbm(T.val[:, (lvl - 1) * K4:lvl * K4]), after=after)

    def rows(name):
        return (T[name][0:128:16, :], [(name, 0, 16 * ROW)])

    def banks(n):
        return [(lo, min(lo + 512, n)) for lo in range(0, n, 512)]

    def sub(x, lo, hi):
        return A(x[0], x[1] + lo, x[1] + hi)

    def level(n, win, off, fac, prod, acc, base, out, sign, gap=None):
        ident = A("idn" if sign < 0 else "idp", 0, 128)
        op = ALU.subtract if sign < 0 else ALU.add
        if base is not None:
            for lo, hi in banks(n):
                mm(A(acc, lo, hi), A("idb", 0, 128), sub(base, lo, hi), True, False)
        third = THIRD if n > 512 else 0
        for e in range(4):
            for lo, hi in ((0, 256), (256, n)) if e == 0 and n > 512 else ((0, n),):
                tt(sub(prod[e], lo, hi), I(win, sub(off(e), lo // 16, hi // 16)), sub(fac(e), lo, hi), ALU.mult)
                for a, b in banks(n):
                    a, b = max(a, lo), min(b, hi, third if e == 2 else n)
                    if e < 3 and a < b:
                        mm(A(acc, a, b), ident, sub(prod[e], a, b), base is None and e == 0, e == 2 or (e == 1 and a >= third))
        tt(A(acc, third, n), A(acc, third, n), sub(prod[2], third, n), op)
        if gap:
            gap()
        for lo, hi in reversed(banks(n)):
            if out is None:
                tt(A(acc, lo, hi), sub(prod[3], lo, hi), A(acc, lo, hi), ALU.subtract)
            else:
                tt(sub(out, lo, hi), A(acc, lo, hi), sub(prod[3], lo, hi), op)

    def positions(lo, hi, between):
        ts(A("qa", lo, hi), A("enti", lo, hi), 63, ALU.bitwise_and)
        between[0]()
        ts(A("qb", lo, hi), A("qa", lo, hi), float(64 * 160 - 1), ALU.mult)
        between[1]()
        tt(A("qb", lo, hi), A("qb", lo, hi), A("enti", lo, hi), ALU.add)
        between[2]()
        ts(A("qu", lo, hi), A("qb", lo, hi), 1.0 / 64, ALU.mult)

    def numbers(k):
        iota(A("num", M * k, M * k + M), [[1, M]], PAD + M * k, 0, True)

    def invert(k, between):
        col = (176 + 44 * k) if k < 4 else 44 * (k - 4)
        for lo, hi in ((0, 22), (22, 44)) if between else ((0, 44),):
            act(I(A("inva" if k < 4 else "invb", 0, 16 * ROW), A("qu", col + lo, col + hi)), A("num", M * k + 16 * lo, M * k + 16 * hi), ACT.Silu)
            if between:
                between.pop(0)()

    def pack(acc, block, width, srcs):
        for s in range(4):
            for k, src in enumerate(srcs):
                mm(A(acc, width * s, width * s + width), A("idp", 0, 128), A(src, 160 * s + block, 160 * s + block + width),
                   k == 0, k == len(srcs) - 1)

    def deal(acc, src):
        for c in range(16):
            mm(A(acc, 0, 56), A("sel", 15 - c, 143 - c), A(src, c, 4 * GH, 16), c == 0, c == 15)

    def links(lk, col):
        steps = []
        for d in range(N - 1):
            o = A("so", col + 2 * d, col + 2 * d + 2)
            if d:
                steps.append(lambda d=d, o=o: act(A(lk, M + S * (d - 1), M + S * d), I(A(lk, 0, M), o), ACT.Copy))
            steps.append(lambda d=d, o=o: act(I(A(lk, 0, M), o), A("num", S * d, S * d + S), ACT.Silu))
        return steps

    def products(col, acc):
        for e in range(4):
            tt(A("pw", col + M * e, col + M * e + M), A("valb", col + M * e, col + M * e + M), A(acc, 0, M), ALU.mult)

    def slot(out, win, off, base):
        if base is None:
            copy(out, I(win, off))
        else:
            tt(out, I(win, off), base, ALU.add)

    def slots(out, win, off, col, width, base, n=4, between=()):
        for s in range(n):
            slot(out, win, A(off, col + s * width, col + (s + 1) * width), base if s == 0 else out)
            if s < len(between):
                between[s]()

    def chain(rc, col, between=()):
        for d in range(1, N - 1):
            x = A(rc, PAD + S * d, PAD + S * d + S)
            tt(x, I(A(rc, 0, PAD + S * d), A("lu", col + 42 + 2 * d, col + 44 + 2 * d)), x, ALU.add)
            if d - 1 < len(between):
                between[d - 1]()

    def last(rc, col, z, lo, hi):
        tt(sub(z, lo, hi), I(A(rc, 0, PAD + GH), A("lu", col + lo // 16, col + hi // 16)), sub(z, lo, hi), ALU.add)

    dma("y", "d_sl", A("sli", 0, 28), hbm(T.sl[:]))
    dma("s", "d_b0", A("wb", 0, M), hbm(T.b[:, 0:M]))
    dma("y", "d_ent", A("enti", 0, 352), hbm(T.ent[:]))
    zeros = fill(A("lk0", 0, M), 0.0)
    dma("y", "d_fa", rows("inva"), A("lk0", 0, ROW))
    for c in range(8):
        spread("s", "d_v1", c, 1, after=[zeros])
        spread("y", "d_v1", c + 8, 1)
    dma("y", "d_b12", A("wb", M, R), hbm(T.b[:, M:R]))
    iota(A("ci", 0, 16), [[1, 16]], 128, -1)
    iota(A("ci", 16, 24), [[-16, 8]], 0, 1)
    iota(A("ci", 24, 152), [[1, 128]], 0, -1)
    numbers(0)
    fill(A("sel", 0, 144), 0.0)
    fill(A("pw", 0, PAD), 0.0)
    fill(A("valb", 0, PAD), 0.0)
    fill(A("r3", 0, PAD), 0.0)
    fill(A("r4", 0, PAD), 0.0)
    ts(A("cj", 0, 16), A("ci", 0, 16), 15, ALU.bitwise_and)
    ts(A("cj", 16, 24), A("ci", 16, 24), 4, ALU.arith_shift_right)
    ts(A("idb", 0, 128), A("ci", 24, 152), 0.0, ALU.is_equal)
    ts(A("idn", 0, 128), A("ci", 24, 152), 0.0, ALU.is_equal, -1.0, ALU.mult)
    ts(A("idp", 0, 128), A("ci", 24, 152), 0.0, ALU.is_equal)
    ts(A("eq", 0, 16), A("cj", 0, 16), 0.0, ALU.is_equal)
    ts(A("sel", 15, 143, 16), A("cj", 16, 24), 0.0, ALU.is_equal)
    act(A("lk1", 0, M), A("lk0", 0, M), ACT.Copy)
    act(A("w", 0, M), A("wb", 0, M), ACT.Copy)

    copy(A("so", 0, 28), A("sli", 0, 28))
    ts(A("so", 28, 42), A("sli", 14, 28), float(-M), ALU.add)
    copy(A("x1", 0, GH), I(A("wb", 0, M), A("so", 0, 14)))
    sent1 = exchange(1, "x1", "wb", R, False)
    steps = links("lk1", 28)
    steps.pop(0)()
    positions(176, 352, [lambda: ts(A("si", 0, 14), A("sli", 14, 28), 4, ALU.arith_shift_right),
                         lambda: ts(A("si", 16, 30), A("sli", 14, 28), 15, ALU.bitwise_and),
                         lambda: copy(A("so", 70, 84), A("si", 16, 30))])
    for k in range(1, 5):
        numbers(k)
    invert(0, steps)
    ts(A("pl", 0, 176), A("enti", 0, 176), 2, ALU.arith_shift_right)
    ts(A("so", 42, 56), A("si", 0, 14), -44.0, ALU.add)
    ts(A("so", 56, 70), A("si", 0, 14), -40.0, ALU.add)
    copy(A("msk", 0, GH), I(A("eq", 0, 16), A("so", 70, 84)))
    ts(A("pl", 176, 352), A("enti", 176, 352), 2, ALU.arith_shift_right)
    for e in range(4):
        odd = e % 2
        tt(A("gm", GH * e, GH * e + GH), I(A("pl", 44 * e - 4 * odd, 44 * e + 44), A("so", 42 + 14 * odd, 56 + 14 * odd)),
           A("msk", 0, GH), ALU.mult)
    deal("accp", "gm")
    positions(0, 176, [lambda: copy(A("plu", 0, 118), A("pl", 0, 118)), lambda: copy(A("plu", 118, 236), A("pl", 118, 236)),
                       lambda: copy(A("plu", 236, 352), A("pl", 236, 352))])
    for e in range(4):
        copy(A("vc", GH * e, GH * e + GH), I(A("valb", V1 + M * e, V1 + M * e + M), A("so", 28, 42)))
    copy(A("bsh", 0, GH), I(A("wb", 0, 2 * M), A("so", 14, 28)))
    for c in range(16):
        spread("y", "d_v2", c, 2, after=[sent1])
    dma("y", "d_fb", rows("invb"), A("lk0", 0, ROW))
    invert(1, steps)

    wbw = A("wb", 0, R + GH)
    copy(A("pcu", 0, 56), A("accp", 0, 56))
    level(GH, wbw, lambda e: ("pcu", 14 * e), lambda e: ("vc", GH * e),
          [("ps", GH * e) for e in range(4)], "accs", ("bsh", 0), ("x2", 0), -1)
    sent2 = exchange(2, "x2", "w", R + GH, False)
    level(M, wbw, lambda e: ("plu", 44 * e), lambda e: ("valb", V1 + M * e),
          [("w", 2 * M)] + [("pr", M * e) for e in range(1, 4)], "acc1", ("wb", M), ("w", M), -1,
          lambda: copy(A("w", R, R + GH), A("wb", R, R + GH)))
    invert(2, steps)
    invert(3, steps)
    dma("y", "d_e1", A("ext", 0, ROW), rows("inva"), after=[sent2])
    for k in range(4, 8):
        if k > 4:
            numbers(k)
        invert(k, steps)

    level(M, A("w", 0, R + 2 * GH), lambda e: ("plu", 176 + 44 * e), lambda e: ("valb", V2 + M * e),
          [("pr", M * e) for e in range(4)], "acc2", ("wb", 2 * M), None, -1)

    pack("accp", 146, 14, ["ext"])
    pack("accr", 44, 44, ["ext"])
    deal("accq", "lk1")
    products(V2, "acc2")
    ts(A("og", 0, 56), A("accp", 0, 56), 0.25, ALU.add)
    slots(A("x3", 0, GH), A("pw", 0, V1), "og", 0, 14, None, between=[
        lambda: ts(A("oo", 0, 88), A("accr", 0, 88), 0.25, ALU.add),
        lambda: ts(A("oo", 88, 176), A("accr", 88, 176), 0.25, ALU.add)])
    sent3 = exchange(3, "x3", "r3", PAD, True)
    dma("y", "d_e0", A("exb", 0, ROW), rows("invb"))
    act(A("zw", 0, M), A("acc2", 0, M), ACT.Copy, -1.0)
    for step in links("lk0", 0):
        step()
    dma("y", "d_z2", hbm(T.z[:, 2 * M:R]), A("zw", 0, M), after=[sent3])
    pack("accp", 132, 14, ["ext", "exb"])
    pack("accr", 0, 44, ["ext", "exb"])
    slots(A("zw", M, 2 * M), A("pw", 0, V1), "oo", 0, 44, A("w", M, 2 * M), between=[
        lambda: None, lambda: None, lambda: ts(A("lu", 0, 56), A("accq", 0, 56), 1.0 / 16, ALU.mult, 0.25, ALU.add)])
    ts(A("og", 56, 112), A("accp", 0, 56), 0.25, ALU.add)
    act(A("vg", 0, 4 * GH), I(A("valb", 0, V1 + K4), A("og", 56, 112)), ACT.Copy, -1.0)
    ts(A("gk", 0, 56), A("accp", 0, 56), 1.0 / M, ALU.mult, (0.5 - PAD) / M - 0.5, ALU.add)
    ts(A("gn", 0, 56), A("accp", 0, 56), V1 - 0.5, ALU.is_ge, float(M), ALU.mult)
    chain("r3", 0, [lambda: ts(A("gn", 56, 112), A("gk", 0, 56), float(-M), ALU.mult, 0.25 - PAD, ALU.add),
                    lambda: tt(A("gn", 0, 56), A("gn", 0, 56), A("accp", 0, 56), ALU.add),
                    lambda: tt(A("gn", 112, 168), A("gn", 0, 56), A("gn", 56, 112), ALU.add),
                    lambda: copy(A("xu", 0, 56), A("gn", 112, 168)),
                    lambda: ts(A("oo", 176, 264), A("accr", 0, 88), 0.25, ALU.add),
                    lambda: ts(A("oo", 264, 352), A("accr", 88, 176), 0.25, ALU.add)])
    last("r3", 0, ("zw", M), 0, M)

    act(A("acc1", 0, M), A("zw", M, 2 * M), ACT.Copy, -1.0)
    level(GH, A("zw", 0, 2 * M), lambda e: ("xu", 14 * e), lambda e: ("vg", GH * e),
          [("ps", GH * e) for e in range(4)], "accs", None, ("x4", 0), 1)
    sent4 = exchange(4, "x4", "r4", PAD, True)
    dma("y", "d_z1", hbm(T.z[:, M:2 * M]), A("zw", M, 2 * M), after=[sent4])
    deal("accq", "lk0")
    products(V1, "acc1")
    pww = A("pw", 0, V1 + K4)
    for lo, hi in banks(M):
        mm(A("acc2", lo, hi), A("idb", 0, 128), A("wb", lo, hi), True, False)
    for s, lo, hi in [(3, 512, M), (2, 0, SHARE), (3, 0, 256), (3, 256, 512)]:
        act(A("pr", M * s + lo, M * s + hi), I(pww, A("oo", 176 + 44 * s + lo // 16, 176 + 44 * s + hi // 16)), ACT.Copy)
        mm(A("acc2", lo, hi), A("idp", 0, 128), A("pr", M * s + lo, M * s + hi), False, s == 3 and hi >= 512)
    slots(A("z0", 0, M), pww, "oo", 176, 44, None, 2,
          between=[lambda: ts(A("lu", 56, 112), A("accq", 0, 56), 1.0 / 16, ALU.mult, 0.25, ALU.add)])
    slot(A("z0", SHARE, M), pww, A("oo", 264 + SHARE // 16, 308), A("z0", SHARE, M))
    tt(A("z0", 0, 256), A("z0", 0, 256), A("acc2", 0, 256), ALU.add)
    chain("r4", 56, [lambda lo=lo: tt(A("z0", lo, lo + 112), A("z0", lo, lo + 112), A("acc2", lo, lo + 112), ALU.add)
                     for lo in range(256, M, 112)])
    H = 448
    last("r4", 56, ("z0", 0), 0, H)
    dma("y", "d_z0", hbm(T.z[:, 0:H]), A("z0", 0, H))
    last("r4", 56, ("z0", 0), H, M)
    dma("s", "d_z0b", hbm(T.z[:, H:M]), A("z0", H, M))
    emit(g, T, ops)
